import numpy as np
import ml_dtypes


def mxq(x, axis, fmt="e4m3"):
    dtype, down = {"e4m3": (ml_dtypes.float8_e4m3fn, 7), "e5m2": (ml_dtypes.float8_e5m2, 14)}[fmt]
    v = np.moveaxis(np.asarray(x, np.float32).astype(ml_dtypes.bfloat16).astype(np.float64), axis, -1)
    blocks = v.reshape(v.shape[:-1] + (-1, 32))
    amax = np.abs(blocks).max(-1, keepdims=True)
    byte = np.maximum(np.where(amax > 0, np.frexp(amax)[1] - 1 + 127, 0) - down, 1)
    scale = np.exp2(byte - 127.0)
    codes = (blocks / scale).astype(np.float32).astype(dtype).astype(np.float64)
    return np.moveaxis((codes * scale).reshape(v.shape), -1, axis)


WIDE = False


def mx_kscale(k):
    if not WIDE:
        return np.ones(k)
    levels = np.array([10, -10, 5, -5, 0])
    if k % 512:
        return np.exp2(np.random.permutation(np.resize(levels, k // 32))).repeat(32)
    a = np.empty((k // 512, 16))
    for p in range(k // 512):
        a[p, :8] = np.random.permutation(np.resize(levels, 8))
        for g in range(8):
            far = levels[np.abs(levels - a[p, g]) >= 10]
            a[p, g + 8] = far[np.random.randint(len(far))]
    return np.exp2(a.ravel()).repeat(32)


def f64(x):
    return np.asarray(x).astype(np.float64)


def striped(idx):
    return np.tile(idx.reshape(-1, 16).T, (8, 1)).astype(np.uint16)


def unstriped(offs):
    return offs[:16].T.reshape(-1).astype(np.int64)


def striped8(idx):
    return np.concatenate([x.reshape(-1, 16).T for x in idx]).astype(np.uint16)


def runs(offs, k):
    lists = np.stack([offs[16 * r : 16 * r + 16].T.reshape(-1) for r in range(8)]).astype(np.int64)
    return lists[np.arange(k) % 512 // 64]


def pack_weight(w):
    k, n = w.shape
    w = f64(np.asarray(w, np.float32).astype(ml_dtypes.bfloat16)).reshape(k // 32, 32, n)
    amax = np.abs(w).max(1)
    byte = np.clip(np.where(amax > 0, np.frexp(amax)[1] - 1 + 127 - 7, 1), 1, 254)
    scaled = (w * np.exp2(127.0 - byte)[:, None, :]).reshape(k, n).astype(np.float32)
    words = np.ascontiguousarray(scaled.reshape(k // 512, 128, 4, n).transpose(0, 1, 3, 2)).astype(ml_dtypes.float8_e4m3fn).view(np.uint8)
    return words, np.ascontiguousarray(byte.astype(np.uint8).reshape(k // 512, 16, n))


def unpack_weight(words, scales):
    g, p, n, _ = words.shape
    vals = np.ascontiguousarray(words).view(ml_dtypes.float8_e4m3fn).astype(np.float64) * np.repeat(np.exp2(scales.astype(np.float64) - 127.0), 8, axis=1)[..., None]
    return vals.transpose(0, 1, 3, 2).reshape(g * 512, n)


E2M1 = np.array([0.0, 0.5, 1.0, 1.5, 2.0, 3.0, 4.0, 6.0, -0.0, -0.5, -1.0, -1.5, -2.0, -3.0, -4.0, -6.0])


def pack_fp4(w):
    k, n = w.shape
    w = f64(np.asarray(w, np.float32).astype(ml_dtypes.bfloat16)).reshape(k // 32, 32, n)
    amax = np.abs(w).max(1)
    mant, ex = np.frexp(amax / 6.0)
    byte = np.clip(np.where(amax > 0, np.where(mant > 0.5, ex, ex - 1) + 127, 1), 1, 254)
    scaled = (w * np.exp2(127.0 - byte)[:, None, :]).reshape(k, n).astype(np.float32)
    c = np.ascontiguousarray(scaled.reshape(k // 512, 128, 4, n).transpose(0, 1, 3, 2)).astype(ml_dtypes.float4_e2m1fn).view(np.uint8) & 0xF
    words = (c[..., 0::2] | (c[..., 1::2] << 4)).reshape(k // 512, 128, 2 * n)
    return np.ascontiguousarray(words), np.ascontiguousarray(byte.astype(np.uint8).reshape(k // 512, 16, n))


def unpack_fp4(words, scales):
    g, _, n = scales.shape
    words = np.ascontiguousarray(words).reshape(g, 128, n, 2)
    nib = np.empty((g, 128, n, 4), np.uint8)
    nib[..., 0::2] = words & 0xF
    nib[..., 1::2] = words >> 4
    vals = E2M1[nib] * np.repeat(np.exp2(scales.astype(np.float64) - 127.0), 8, axis=1)[..., None]
    return vals.transpose(0, 1, 3, 2).reshape(g * 512, n)


def planes(y):
    n, m = y.shape
    v = y.astype(np.float32).astype(ml_dtypes.bfloat16).astype(np.float64).reshape(n // 32, 32, m)
    top = np.abs(v).max(1)
    byte = np.clip(np.where(top > 0, np.frexp(top)[1] - 1 + 127 - 7, 1), 1, 254)
    codes = (v * np.exp2(127.0 - byte)[:, None, :]).reshape(n, m).astype(np.float32).astype(ml_dtypes.float8_e4m3fn).view(np.uint8)
    words = codes.reshape(n // 512, 128, 4, m).transpose(0, 1, 3, 2)
    return np.ascontiguousarray(words), np.ascontiguousarray(byte.astype(np.uint8).reshape(n // 512, 16, m))


K, T, S, H, W, C = 512, 2048, 256, 512, 1024, 512


def setup_inputs():
    n = np.random.standard_normal
    s = mx_kscale(K)[:, None]
    packed_xT = pack_weight(n((K, T)) * s)
    packed_w1 = pack_fp4(n((K, H)) / np.sqrt(K) / s)
    return {
        "x_words": packed_xT[0],
        "x_scales": packed_xT[1],
        "w1_words": packed_w1[0],
        "w1_scales": packed_w1[1],
        "gs": (np.random.uniform(0.5, 1.5, (K, 1)) / s).astype(np.float32),
        "wb": (n((K, S)) / np.sqrt(K) / s).astype(np.float32),
        "offs": striped(np.random.permutation(T)[:S]),
        "n1": striped(np.random.randint(0, S, W)),
        "cand": striped(np.random.permutation(T)[:C]),
        "cb": striped(np.random.permutation(T)[:C]),
        "n2": striped8(np.stack([np.random.permutation(S) for _ in range(8)])),
        "n3": striped8(np.stack([np.random.permutation(S) for _ in range(8)])),
        "n4": striped8(np.stack([np.random.permutation(S) for _ in range(8)])),
    }


def reference(x_words, x_scales, w1_words, w1_scales, gs, wb, offs, n1, cand, cb, n2, n3, n4):
    x_cand = unpack_weight(x_words, x_scales)[:, unstriped(cand)]
    xq = unpack_weight(x_words, x_scales)[:, unstriped(offs)]
    y = unpack_fp4(w1_words, w1_scales).T @ xq
    mb = y[:, unstriped(n1)]
    mn = mb.reshape(H, S, 4).min(axis=2)
    mx = mb.reshape(H, S, 4).max(axis=2)
    z = f64(gs) * (np.maximum(y, mn) - (0.5 * mx))
    a = 0.0625 * ((x_cand.T @ mxq(z, 0, "e4m3")))
    x_cb = unpack_weight(x_words, x_scales)[:, unstriped(cb)]
    b = x_cb.T @ mxq(f64(wb), 0, "e4m3")
    out_0 = np.maximum(np.minimum(a - (0.5 * (a[np.arange(C)[:, None], runs(n2, C)])), b[np.arange(C)[:, None], runs(n3, C)]), b[np.arange(C)[:, None], runs(n4, C)])
    return (out_0,) + planes(out_0)

@@ -1,0 +1,238 @@
+from contextlib import ExitStack
+
+import concourse.mybir as mybir
+
+K, T, S, H, W, C = 512, 2048, 256, 512, 1024, 512
+FLOPS = 2 * K * S * (H + 2 * C)
+
+F32 = mybir.dt.float32
+BF16 = mybir.dt.bfloat16
+I32 = mybir.dt.int32
+U32 = mybir.dt.uint32
+U16 = mybir.dt.uint16
+U8 = mybir.dt.uint8
+FP8X4 = mybir.dt.float8_e4m3fn_x4
+FP4X4 = mybir.dt.float4_e2m1fn_x4
+COPY = mybir.ActivationFunctionType.Copy
+ALU = mybir.AluOpType
+
+P = 128
+PACK = 4
+HALF = S // 2
+Y_WINDOW = 528
+AB_WINDOW = 512
+
+
+def tile_picked_cdswclampbgmid_none_po_kernel(
+    tc, x_words, x_scales, w1_words, w1_scales, gs, wb, offs, n1, cand, cb, n2, n3, n4, out_0, out_1, out_2
+):
+    nc = tc.nc
+    with ExitStack() as ctx:
+        sb = ctx.enter_context(tc.tile_pool(name="sb", bufs=1))
+        ps = ctx.enter_context(tc.psum_pool(name="ps", bufs=1))
+
+        def tile(shape, dtype, name):
+            return sb.tile(shape, dtype, name=name, align_bytes=64)
+
+        def load_list(src, name):
+            dst = tile([P, src.shape[1]], U16, name)
+            nc.sync.dma_start(dst[:], src)
+            return dst
+
+        def load_scale_rows(queue, dst, src):
+            for q in range(4):
+                rows = src[0][4 * q : 4 * q + 4, :].bitcast(I32)
+                queue.dma_start(out=dst[32 * q : 32 * (q + 1), :].bitcast(I32), in_=rows.partition_broadcast(8))
+
+        w1_sc = tile([P, H], U8, "w1_sc")
+        load_scale_rows(nc.scalar, w1_sc, w1_scales)
+        offs_l = load_list(offs, "offs_l")
+        cb_l = load_list(cb, "cb_l")
+        w1_w = tile([P, 2 * H], U8, "w1_w")
+        nc.sync.dma_start(out=w1_w[:].bitcast(I32), in_=w1_words[0].bitcast(I32))
+        x_w = tile([P, T], U32, "x_w")
+        nc.sync.dma_start(out=x_w[:].bitcast(I32), in_=x_words[0].rearrange("p n t -> p (n t)").bitcast(I32))
+        x_sc = tile([P, T], U8, "x_sc")
+        load_scale_rows(nc.sync, x_sc, x_scales)
+        wb_raw = tile([P, PACK, S], F32, "wb_raw")
+        nc.sync.dma_start(out=wb_raw[:], in_=wb.rearrange("(p t) j -> p t j", t=PACK))
+        n1_l = load_list(n1, "n1_l")
+        cand_l = load_list(cand, "cand_l")
+        gs_t = tile([P, 1, PACK], F32, "gs_t")
+        nc.sync.dma_start(out=gs_t[:], in_=gs.rearrange("(p t) o -> p o t", t=PACK))
+        n3_l = load_list(n3, "n3_l")
+        n4_l = load_list(n4, "n4_l")
+        n2_l = load_list(n2, "n2_l")
+
+        y_win = [tile([P, Y_WINDOW], F32, f"y_win{t}") for t in range(PACK)]
+        a_win = [tile([P, AB_WINDOW], F32, f"a_win{t}") for t in range(PACK)]
+        b_win = [tile([P, AB_WINDOW], F32, f"b_win{t}") for t in range(PACK)]
+        for win in y_win + b_win + a_win:
+            nc.gpsimd.memset(win[:, S:], 0.0)
+
+        w1_wd = tile([P, 2 * H], U8, "w1_wd")
+        nc.vector.tensor_copy(
+            out=w1_wd[:].rearrange("p (t m b) -> p t m b", t=PACK, b=2),
+            in_=w1_w[:].rearrange("p (m t b) -> p t m b", t=PACK, b=2),
+        )
+        w1_sd = tile([P, H], U8, "w1_sd")
+        nc.vector.tensor_copy(
+            out=w1_sd[:].rearrange("p (t m) -> p t m", t=PACK), in_=w1_sc[:].rearrange("p (m t) -> p t m", t=PACK)
+        )
+
+        def pick(lst, n, name):
+            words = tile([P, n], U32, name + "_w")
+            nc.vector.tensor_copy(out=words[:], in_=x_w[:].indirect(lst[:]))
+            scales = tile([P, n], U8, name + "_s")
+            nc.vector.tensor_copy(out=scales[:], in_=x_sc[:].indirect(lst[:]))
+            return words, scales
+
+        def deal(src, dtype, name):
+            dst = tile([P, C], dtype, name)
+            nc.vector.tensor_copy(
+                out=dst[:].rearrange("p (t m) -> p t m", t=PACK), in_=src[:].rearrange("p (m t) -> p t m", t=PACK)
+            )
+            return dst
+
+        xq_w, xq_s = pick(offs_l, S, "xq")
+        y_ps = [ps.tile([P, 2, S], F32, name=f"y_ps{q}") for q in range(2)]
+        for t in range(PACK):
+            nc.tensor.matmul_mx(
+                out=y_ps[t // 2][:, t % 2, :],
+                lhsT=w1_wd[:, 2 * P * t : 2 * P * (t + 1)].bitcast(FP4X4),
+                lhsT_scale=w1_sd[:, P * t : P * (t + 1)],
+                rhs=xq_w[:].bitcast(FP8X4),
+                rhs_scale=xq_s[:],
+                start=True,
+                stop=True,
+            )
+
+        cb_w, cb_s = pick(cb_l, C, "cb")
+        cb_wd = deal(cb_w, U32, "cb_wd")
+        cb_sd = deal(cb_s, U8, "cb_sd")
+        wb_bf = tile([P, S, PACK], BF16, "wb_bf")
+        nc.scalar.copy(out=wb_bf[:], in_=wb_raw[:].rearrange("p t j -> p j t"))
+        cand_w, cand_s = pick(cand_l, C, "cand")
+        wb_w = tile([P, S], U32, "wb_w")
+        wb_s = tile([P, S], U8, "wb_s")
+        nc.vector.quantize_mx(out=wb_w[:].bitcast(FP8X4), scales=wb_s[:], in_=wb_bf[:].rearrange("p j t -> p (j t)"))
+        b_ps = [ps.tile([P, 2, S], F32, name=f"b_ps{q}") for q in range(2)]
+        for t in range(PACK):
+            nc.tensor.matmul_mx(
+                out=b_ps[t // 2][:, t % 2, :],
+                lhsT=cb_wd[:, P * t : P * (t + 1)].bitcast(FP8X4),
+                lhsT_scale=cb_sd[:, P * t : P * (t + 1)],
+                rhs=wb_w[:].bitcast(FP8X4),
+                rhs_scale=wb_s[:],
+                start=True,
+                stop=True,
+            )
+        cand_wd = deal(cand_w, U32, "cand_wd")
+        cand_sd = deal(cand_s, U8, "cand_sd")
+
+        a_ps = [[ps.tile([P, 2, HALF], F32, name=f"a_ps{h}{q}") for q in range(2)] for h in range(2)]
+        for h in range(2):
+            cols = slice(HALF * h, HALF * (h + 1))
+            u = tile([P, PACK, HALF], F32, f"u{h}")
+            top = tile([P, PACK, HALF], F32, f"top{h}")
+            mx = tile([P, PACK, HALF], F32, f"mx{h}")
+            for q in range(2):
+                pair = slice(2 * q, 2 * q + 2)
+                mb = tile([P, 2, 4 * HALF], F32, f"mb{h}{q}")
+                for e in range(2):
+                    t = 2 * q + e
+                    if h == 0:
+                        nc.scalar.copy(out=y_win[t][:, :S], in_=y_ps[q][:, e, :])
+                    nc.scalar.activation(out=mb[:, e, :], in_=y_win[t][:].indirect(n1_l[:, 32 * h : 32 * (h + 1)]), func=COPY)
+                members = mb[:].rearrange("p e (j m) -> p (e j) m", m=4)
+                lo = tile([P, S, 2], F32, f"lo{h}{q}")
+                hi = tile([P, S, 2], F32, f"hi{h}{q}")
+                mn = tile([P, 2, HALF], F32, f"mn{h}{q}")
+                nc.vector.tensor_tensor(out=lo[:], in0=members[:, :, 0:2], in1=members[:, :, 2:4], op=ALU.min)
+                nc.vector.tensor_tensor(out=hi[:], in0=members[:, :, 0:2], in1=members[:, :, 2:4], op=ALU.max)
+                nc.vector.tensor_tensor(
+                    out=mn[:].rearrange("p e j -> p (e j)"), in0=lo[:, :, 0], in1=lo[:, :, 1], op=ALU.min
+                )
+                nc.vector.tensor_tensor(
+                    out=mx[:, pair, :].rearrange("p e j -> p (e j)"), in0=hi[:, :, 0], in1=hi[:, :, 1], op=ALU.max
+                )
+                nc.vector.tensor_tensor(out=top[:, pair, :], in0=y_ps[q][:, :, cols], in1=mn[:], op=ALU.max)
+            nc.vector.scalar_tensor_tensor(
+                out=u[:], in0=mx[:], scalar=-0.5, in1=top[:], op0=ALU.mult, op1=ALU.add
+            )
+            z_bf = tile([P, HALF, PACK], BF16, f"z_bf{h}")
+            nc.vector.tensor_tensor(
+                out=z_bf[:],
+                in0=u[:].rearrange("p t j -> p j t"),
+                in1=gs_t[:].to_broadcast([P, HALF, PACK]),
+                op=ALU.mult,
+            )
+            z_w = tile([P, HALF], U32, f"z_w{h}")
+            z_s = tile([P, HALF], U8, f"z_s{h}")
+            nc.vector.quantize_mx(out=z_w[:].bitcast(FP8X4), scales=z_s[:], in_=z_bf[:].rearrange("p j t -> p (j t)"))
+            for t in range(PACK):
+                nc.tensor.matmul_mx(
+                    out=a_ps[h][t // 2][:, t % 2, :],
+                    lhsT=cand_wd[:, P * t : P * (t + 1)].bitcast(FP8X4),
+                    lhsT_scale=cand_sd[:, P * t : P * (t + 1)],
+                    rhs=z_w[:].bitcast(FP8X4),
+                    rhs_scale=z_s[:],
+                    start=True,
+                    stop=True,
+                )
+
+        g3 = tile([P, PACK, S], F32, "g3")
+        g4 = tile([P, PACK, S], F32, "g4")
+        for t in range(PACK):
+            nc.scalar.copy(out=b_win[t][:, :S], in_=b_ps[t // 2][:, t % 2, :])
+            nc.scalar.activation(out=g3[:, t, :], in_=b_win[t][:].indirect(n3_l[:]), func=COPY)
+            nc.scalar.activation(out=g4[:, t, :], in_=b_win[t][:].indirect(n4_l[:]), func=COPY)
+
+        for h in range(2):
+            cols = slice(HALF * h, HALF * (h + 1))
+            for t in range(PACK):
+                if h == 1 and t >= 2:
+                    nc.vector.tensor_copy(out=a_win[t][:, cols], in_=a_ps[h][t // 2][:, t % 2, :])
+                else:
+                    nc.scalar.copy(out=a_win[t][:, cols], in_=a_ps[h][t // 2][:, t % 2, :])
+
+        out_rows = out_0.rearrange("(p t) j -> p t j", t=PACK)
+        out_words = out_1[0].rearrange("p n t -> p (n t)")
+        o_w = tile([P, S], U32, "o_w")
+        o_s = tile([P, S], U8, "o_s")
+        for h in range(2):
+            cols = slice(HALF * h, HALF * (h + 1))
+            res = tile([P, PACK, HALF], F32, f"res{h}")
+            for q in range(2):
+                pair = slice(2 * q, 2 * q + 2)
+                g2 = tile([P, 2, HALF], F32, f"g2{h}{q}")
+                for e in range(2):
+                    nc.scalar.activation(
+                        out=g2[:, e, :], in_=a_win[2 * q + e][:].indirect(n2_l[:, 8 * h : 8 * (h + 1)]), func=COPY
+                    )
+                diff = tile([P, 2, HALF], F32, f"diff{h}{q}")
+                nc.vector.scalar_tensor_tensor(
+                    out=diff[:], in0=g2[:], scalar=-0.5, in1=a_ps[h][q][:], op0=ALU.mult, op1=ALU.add
+                )
+                low = tile([P, 2, HALF], F32, f"low{h}{q}")
+                nc.vector.scalar_tensor_tensor(
+                    out=low[:], in0=diff[:], scalar=0.0625, in1=g3[:, pair, cols], op0=ALU.mult, op1=ALU.min
+                )
+                nc.vector.tensor_tensor(out=res[:, pair, :], in0=low[:], in1=g4[:, pair, cols], op=ALU.max)
+                nc.sync.dma_start(out=out_rows[:, pair, cols], in_=res[:, pair, :])
+            o_bf = tile([P, HALF, PACK], BF16, f"o_bf{h}")
+            if h == 0:
+                nc.scalar.copy(out=o_bf[:], in_=res[:].rearrange("p t j -> p j t"))
+            else:
+                nc.vector.tensor_copy(out=o_bf[:], in_=res[:].rearrange("p t j -> p j t"))
+            nc.vector.quantize_mx(
+                out=o_w[:, cols].bitcast(FP8X4), scales=o_s[:, cols], in_=o_bf[:].rearrange("p j t -> p (j t)")
+            )
+            nc.sync.dma_start(
+                out=out_words[:, 4 * HALF * h : 4 * HALF * (h + 1)].bitcast(I32), in_=o_w[:, cols].bitcast(I32)
+            )
+        for q in range(4):
+            queue = nc.sync if q % 2 == 0 else nc.scalar
+            queue.dma_start(
+                out=out_2[0][4 * q : 4 * q + 4, :].bitcast(I32), in_=o_s[32 * q : 32 * q + 4, :].bitcast(I32)
+            )

@@ -20,7 +20,7 @@ P = 128
 PACK = 4
 HALF = S // 2
 Y_WINDOW = 528
-AB_WINDOW = 512
+B_WINDOW = 512
 
 
 def tile_picked_cdswclampbgmid_none_po_kernel(
@@ -31,70 +31,77 @@ def tile_picked_cdswclampbgmid_none_po_kernel(
         sb = ctx.enter_context(tc.tile_pool(name="sb", bufs=1))
         ps = ctx.enter_context(tc.psum_pool(name="ps", bufs=1))
 
-        def tile(shape, dtype, name):
-            return sb.tile(shape, dtype, name=name, align_bytes=64)
+        def tile(shape, dtype, name, tag=None):
+            return sb.tile(shape, dtype, name=name, tag=tag or name, align_bytes=64)
 
         def load_list(src, name):
             dst = tile([P, src.shape[1]], U16, name)
             nc.sync.dma_start(dst[:], src)
             return dst
 
-        def load_scale_rows(queue, dst, src):
+        def load_scale_rows(dst, src):
             for q in range(4):
                 rows = src[0][4 * q : 4 * q + 4, :].bitcast(I32)
-                queue.dma_start(out=dst[32 * q : 32 * (q + 1), :].bitcast(I32), in_=rows.partition_broadcast(8))
+                nc.sync.dma_start(out=dst[32 * q : 32 * (q + 1), :].bitcast(I32), in_=rows.partition_broadcast(8))
 
-        w1_sc = tile([P, H], U8, "w1_sc")
-        load_scale_rows(nc.scalar, w1_sc, w1_scales)
+        x_sc = tile([P, T], U8, "x_sc")
+        load_scale_rows(x_sc, x_scales)
         offs_l = load_list(offs, "offs_l")
         cb_l = load_list(cb, "cb_l")
         w1_w = tile([P, 2 * H], U8, "w1_w")
         nc.sync.dma_start(out=w1_w[:].bitcast(I32), in_=w1_words[0].bitcast(I32))
         x_w = tile([P, T], U32, "x_w")
         nc.sync.dma_start(out=x_w[:].bitcast(I32), in_=x_words[0].rearrange("p n t -> p (n t)").bitcast(I32))
-        x_sc = tile([P, T], U8, "x_sc")
-        load_scale_rows(nc.sync, x_sc, x_scales)
-        wb_raw = tile([P, PACK, S], F32, "wb_raw")
-        nc.sync.dma_start(out=wb_raw[:], in_=wb.rearrange("(p t) j -> p t j", t=PACK))
+        w1_sc = tile([P, H], U8, "w1_sc")
+        load_scale_rows(w1_sc, w1_scales)
         n1_l = load_list(n1, "n1_l")
         cand_l = load_list(cand, "cand_l")
-        gs_t = tile([P, 1, PACK], F32, "gs_t")
-        nc.sync.dma_start(out=gs_t[:], in_=gs.rearrange("(p t) o -> p o t", t=PACK))
+        gs_t = tile([P, 1, PACK, 1], F32, "gs_t")
+        nc.sync.dma_start(out=gs_t[:, 0, :, :], in_=gs.rearrange("(p t) o -> p t o", t=PACK))
+        wb_raw = tile([P, PACK, S], F32, "wb_raw")
+        nc.sync.dma_start(out=wb_raw[:], in_=wb.rearrange("(p t) j -> p t j", t=PACK))
         n3_l = load_list(n3, "n3_l")
         n4_l = load_list(n4, "n4_l")
         n2_l = load_list(n2, "n2_l")
 
         y_win = [tile([P, Y_WINDOW], F32, f"y_win{t}") for t in range(PACK)]
-        a_win = [tile([P, AB_WINDOW], F32, f"a_win{t}") for t in range(PACK)]
-        b_win = [tile([P, AB_WINDOW], F32, f"b_win{t}") for t in range(PACK)]
-        for win in y_win + b_win + a_win:
+        a_win = [tile([P, S], F32, f"a_win{t}") for t in range(PACK)]
+        b_win = [tile([P, B_WINDOW], F32, f"b_win{t}") for t in range(PACK)]
+        for win in y_win + b_win:
             nc.gpsimd.memset(win[:, S:], 0.0)
 
+        def pick(table, lst, n, dtype, name, tag=None):
+            dst = tile([P, n], dtype, name, tag)
+            nc.vector.tensor_copy(out=dst[:], in_=table[:].indirect(lst[:]))
+            return dst
+
+        def pick_dealt(lst, name, tag=None):
+            dst = tile([P, C], U32, name, tag)
+            nc.vector.tensor_copy(out=dst[:].rearrange("p (t m) -> p m t", t=PACK), in_=x_w[:].indirect(lst[:]))
+            return dst
+
+        def deal(src, dtype, run, name):
+            dst = tile([P, C], dtype, name)
+            nc.vector.tensor_copy(
+                out=dst[:].rearrange("p (t c i) -> p c t i", t=PACK, i=run),
+                in_=src[:].rearrange("p (c i t) -> p c t i", t=PACK, i=run),
+            )
+            return dst
+
+        def woven(dst):
+            return dst[:].rearrange("p (c i) t -> p c t i", i=4)
+
+        def by_runs(src):
+            return src[:].rearrange("p t (c i) -> p c t i", i=4)
+
+        xq_s = pick(x_sc, offs_l, S, U8, "xq_s")
         w1_wd = tile([P, 2 * H], U8, "w1_wd")
         nc.vector.tensor_copy(
             out=w1_wd[:].rearrange("p (t m b) -> p t m b", t=PACK, b=2),
             in_=w1_w[:].rearrange("p (m t b) -> p t m b", t=PACK, b=2),
         )
-        w1_sd = tile([P, H], U8, "w1_sd")
-        nc.vector.tensor_copy(
-            out=w1_sd[:].rearrange("p (t m) -> p t m", t=PACK), in_=w1_sc[:].rearrange("p (m t) -> p t m", t=PACK)
-        )
-
-        def pick(lst, n, name):
-            words = tile([P, n], U32, name + "_w")
-            nc.vector.tensor_copy(out=words[:], in_=x_w[:].indirect(lst[:]))
-            scales = tile([P, n], U8, name + "_s")
-            nc.vector.tensor_copy(out=scales[:], in_=x_sc[:].indirect(lst[:]))
-            return words, scales
-
-        def deal(src, dtype, name):
-            dst = tile([P, C], dtype, name)
-            nc.vector.tensor_copy(
-                out=dst[:].rearrange("p (t m) -> p t m", t=PACK), in_=src[:].rearrange("p (m t) -> p t m", t=PACK)
-            )
-            return dst
-
-        xq_w, xq_s = pick(offs_l, S, "xq")
+        xq_w = pick(x_w, offs_l, S, U32, "xq_w")
+        w1_sd = deal(w1_sc, U8, 16, "w1_sd")
         y_ps = [ps.tile([P, 2, S], F32, name=f"y_ps{q}") for q in range(2)]
         for t in range(PACK):
             nc.tensor.matmul_mx(
@@ -106,13 +113,15 @@ def tile_picked_cdswclampbgmid_none_po_kernel(
                 start=True,
                 stop=True,
             )
+            nc.scalar.copy(out=y_win[t][:, :S], in_=y_ps[t // 2][:, t % 2, :])
 
-        cb_w, cb_s = pick(cb_l, C, "cb")
-        cb_wd = deal(cb_w, U32, "cb_wd")
-        cb_sd = deal(cb_s, U8, "cb_sd")
+        cb_s = pick(x_sc, cb_l, C, U8, "cb_s")
+        cb_wd = pick_dealt(cb_l, "cb_wd", tag="w1_sc")
+        cb_sd = deal(cb_s, U8, 16, "cb_sd")
         wb_bf = tile([P, S, PACK], BF16, "wb_bf")
-        nc.scalar.copy(out=wb_bf[:], in_=wb_raw[:].rearrange("p t j -> p j t"))
-        cand_w, cand_s = pick(cand_l, C, "cand")
+        nc.vector.tensor_copy(out=woven(wb_bf), in_=by_runs(wb_raw))
+        cand_s = pick(x_sc, cand_l, C, U8, "cand_s")
+        cand_wd = pick_dealt(cand_l, "cand_wd")
         wb_w = tile([P, S], U32, "wb_w")
         wb_s = tile([P, S], U8, "wb_s")
         nc.vector.quantize_mx(out=wb_w[:].bitcast(FP8X4), scales=wb_s[:], in_=wb_bf[:].rearrange("p j t -> p (j t)"))
@@ -127,8 +136,7 @@ def tile_picked_cdswclampbgmid_none_po_kernel(
                 start=True,
                 stop=True,
             )
-        cand_wd = deal(cand_w, U32, "cand_wd")
-        cand_sd = deal(cand_s, U8, "cand_sd")
+        cand_sd = deal(cand_s, U8, 16, "cand_sd")
 
         a_ps = [[ps.tile([P, 2, HALF], F32, name=f"a_ps{h}{q}") for q in range(2)] for h in range(2)]
         for h in range(2):
@@ -141,8 +149,6 @@ def tile_picked_cdswclampbgmid_none_po_kernel(
                 mb = tile([P, 2, 4 * HALF], F32, f"mb{h}{q}")
                 for e in range(2):
                     t = 2 * q + e
-                    if h == 0:
-                        nc.scalar.copy(out=y_win[t][:, :S], in_=y_ps[q][:, e, :])
                     nc.scalar.activation(out=mb[:, e, :], in_=y_win[t][:].indirect(n1_l[:, 32 * h : 32 * (h + 1)]), func=COPY)
                 members = mb[:].rearrange("p e (j m) -> p (e j) m", m=4)
                 lo = tile([P, S, 2], F32, f"lo{h}{q}")
@@ -162,9 +168,9 @@ def tile_picked_cdswclampbgmid_none_po_kernel(
             )
             z_bf = tile([P, HALF, PACK], BF16, f"z_bf{h}")
             nc.vector.tensor_tensor(
-                out=z_bf[:],
-                in0=u[:].rearrange("p t j -> p j t"),
-                in1=gs_t[:].to_broadcast([P, HALF, PACK]),
+                out=woven(z_bf),
+                in0=by_runs(u),
+                in1=gs_t[:].to_broadcast([P, HALF // 4, PACK, 4]),
                 op=ALU.mult,
             )
             z_w = tile([P, HALF], U32, f"z_w{h}")
@@ -191,7 +197,7 @@ def tile_picked_cdswclampbgmid_none_po_kernel(
         for h in range(2):
             cols = slice(HALF * h, HALF * (h + 1))
             for t in range(PACK):
-                if h == 1 and t >= 2:
+                if (h, t) in ((0, 2), (0, 3), (1, 2), (1, 3)):
                     nc.vector.tensor_copy(out=a_win[t][:, cols], in_=a_ps[h][t // 2][:, t % 2, :])
                 else:
                     nc.scalar.copy(out=a_win[t][:, cols], in_=a_ps[h][t // 2][:, t % 2, :])
@@ -222,9 +228,9 @@ def tile_picked_cdswclampbgmid_none_po_kernel(
                 nc.sync.dma_start(out=out_rows[:, pair, cols], in_=res[:, pair, :])
             o_bf = tile([P, HALF, PACK], BF16, f"o_bf{h}")
             if h == 0:
-                nc.scalar.copy(out=o_bf[:], in_=res[:].rearrange("p t j -> p j t"))
+                nc.scalar.copy(out=woven(o_bf), in_=by_runs(res))
             else:
-                nc.vector.tensor_copy(out=o_bf[:], in_=res[:].rearrange("p t j -> p j t"))
+                nc.vector.tensor_copy(out=woven(o_bf), in_=by_runs(res))
             nc.vector.quantize_mx(
                 out=o_w[:, cols].bitcast(FP8X4), scales=o_s[:, cols], in_=o_bf[:].rearrange("p j t -> p (j t)")
             )

@@ -56,8 +56,8 @@ def tile_picked_cdswclampbgmid_none_po_kernel(
         load_scale_rows(w1_sc, w1_scales)
         n1_l = load_list(n1, "n1_l")
         cand_l = load_list(cand, "cand_l")
-        gs_t = tile([P, 1, PACK, 1], F32, "gs_t")
-        nc.sync.dma_start(out=gs_t[:, 0, :, :], in_=gs.rearrange("(p t) o -> p t o", t=PACK))
+        gs_t = tile([P, 1, PACK], F32, "gs_t")
+        nc.sync.dma_start(out=gs_t[:], in_=gs.rearrange("(p t) o -> p o t", t=PACK))
         wb_raw = tile([P, PACK, S], F32, "wb_raw")
         nc.sync.dma_start(out=wb_raw[:], in_=wb.rearrange("(p t) j -> p t j", t=PACK))
         n3_l = load_list(n3, "n3_l")
@@ -65,9 +65,11 @@ def tile_picked_cdswclampbgmid_none_po_kernel(
         n2_l = load_list(n2, "n2_l")
 
         y_win = [tile([P, Y_WINDOW], F32, f"y_win{t}") for t in range(PACK)]
-        a_win = [tile([P, S], F32, f"a_win{t}") for t in range(PACK)]
+        a_win = [tile([P, B_WINDOW], F32, f"a_win{t}") for t in range(PACK)]
         b_win = [tile([P, B_WINDOW], F32, f"b_win{t}") for t in range(PACK)]
         for win in y_win + b_win:
+            nc.vector.memset(win[:, S:], 0.0)
+        for win in a_win:
             nc.gpsimd.memset(win[:, S:], 0.0)
 
         def pick(table, lst, n, dtype, name, tag=None):
@@ -75,24 +77,17 @@ def tile_picked_cdswclampbgmid_none_po_kernel(
             nc.vector.tensor_copy(out=dst[:], in_=table[:].indirect(lst[:]))
             return dst
 
-        def pick_dealt(lst, name, tag=None):
-            dst = tile([P, C], U32, name, tag)
-            nc.vector.tensor_copy(out=dst[:].rearrange("p (t m) -> p m t", t=PACK), in_=x_w[:].indirect(lst[:]))
-            return dst
-
-        def deal(src, dtype, run, name):
-            dst = tile([P, C], dtype, name)
+        def deal(src, dtype, run, name, slots=slice(0, PACK), tag=None):
+            count = slots.stop - slots.start
+            dst = tile([P, count * P], dtype, name, tag)
             nc.vector.tensor_copy(
-                out=dst[:].rearrange("p (t c i) -> p c t i", t=PACK, i=run),
-                in_=src[:].rearrange("p (c i t) -> p c t i", t=PACK, i=run),
+                out=dst[:].rearrange("p (t c i) -> p c t i", t=count, i=run),
+                in_=src[:].rearrange("p (c i t) -> p c t i", t=PACK, i=run)[:, :, slots, :],
             )
             return dst
 
-        def woven(dst):
-            return dst[:].rearrange("p (c i) t -> p c t i", i=4)
-
-        def by_runs(src):
-            return src[:].rearrange("p t (c i) -> p c t i", i=4)
+        def by_column(src):
+            return src[:].rearrange("p t j -> p j t")
 
         xq_s = pick(x_sc, offs_l, S, U8, "xq_s")
         w1_wd = tile([P, 2 * H], U8, "w1_wd")
@@ -116,12 +111,13 @@ def tile_picked_cdswclampbgmid_none_po_kernel(
             nc.scalar.copy(out=y_win[t][:, :S], in_=y_ps[t // 2][:, t % 2, :])
 
         cb_s = pick(x_sc, cb_l, C, U8, "cb_s")
-        cb_wd = pick_dealt(cb_l, "cb_wd", tag="w1_sc")
+        cb_w = pick(x_w, cb_l, C, U32, "cb_w", tag="w1_sc")
         cb_sd = deal(cb_s, U8, 16, "cb_sd")
+        cb_wd = deal(cb_w, U32, 4, "cb_wd")
         wb_bf = tile([P, S, PACK], BF16, "wb_bf")
-        nc.vector.tensor_copy(out=woven(wb_bf), in_=by_runs(wb_raw))
+        nc.vector.tensor_copy(out=wb_bf[:], in_=by_column(wb_raw))
         cand_s = pick(x_sc, cand_l, C, U8, "cand_s")
-        cand_wd = pick_dealt(cand_l, "cand_wd")
+        cand_w = pick(x_w, cand_l, C, U32, "cand_w")
         wb_w = tile([P, S], U32, "wb_w")
         wb_s = tile([P, S], U8, "wb_s")
         nc.vector.quantize_mx(out=wb_w[:].bitcast(FP8X4), scales=wb_s[:], in_=wb_bf[:].rearrange("p j t -> p (j t)"))
@@ -136,9 +132,13 @@ def tile_picked_cdswclampbgmid_none_po_kernel(
                 start=True,
                 stop=True,
             )
-        cand_sd = deal(cand_s, U8, 16, "cand_sd")
+        cand_wd = deal(cand_w, U32, 4, "cand_wd", slice(0, 2))
+        cand_sd = deal(cand_s, U8, 16, "cand_sd", slice(0, 2))
+        z_w = tile([P, S], U32, "z_w")
+        z_s = tile([P, S], U8, "z_s")
 
-        a_ps = [[ps.tile([P, 2, HALF], F32, name=f"a_ps{h}{q}") for q in range(2)] for h in range(2)]
+        a_first = ps.tile([P, 2, HALF], F32, name="a_first")
+        a_ps = [[a_first[:, t, :] for t in range(2)], [ps.tile([P, HALF], F32, name=f"a_second{t}")[:] for t in range(2)]]
         for h in range(2):
             cols = slice(HALF * h, HALF * (h + 1))
             u = tile([P, PACK, HALF], F32, f"u{h}")
@@ -168,24 +168,37 @@ def tile_picked_cdswclampbgmid_none_po_kernel(
             )
             z_bf = tile([P, HALF, PACK], BF16, f"z_bf{h}")
             nc.vector.tensor_tensor(
-                out=woven(z_bf),
-                in0=by_runs(u),
-                in1=gs_t[:].to_broadcast([P, HALF // 4, PACK, 4]),
+                out=z_bf[:],
+                in0=by_column(u),
+                in1=gs_t[:].to_broadcast([P, HALF, PACK]),
                 op=ALU.mult,
             )
-            z_w = tile([P, HALF], U32, f"z_w{h}")
-            z_s = tile([P, HALF], U8, f"z_s{h}")
-            nc.vector.quantize_mx(out=z_w[:].bitcast(FP8X4), scales=z_s[:], in_=z_bf[:].rearrange("p j t -> p (j t)"))
-            for t in range(PACK):
+            nc.vector.quantize_mx(
+                out=z_w[:, cols].bitcast(FP8X4), scales=z_s[:, cols], in_=z_bf[:].rearrange("p j t -> p (j t)")
+            )
+            for t in range(2):
                 nc.tensor.matmul_mx(
-                    out=a_ps[h][t // 2][:, t % 2, :],
+                    out=a_ps[h][t],
                     lhsT=cand_wd[:, P * t : P * (t + 1)].bitcast(FP8X4),
                     lhsT_scale=cand_sd[:, P * t : P * (t + 1)],
-                    rhs=z_w[:].bitcast(FP8X4),
-                    rhs_scale=z_s[:],
+                    rhs=z_w[:, cols].bitcast(FP8X4),
+                    rhs_scale=z_s[:, cols],
                     start=True,
                     stop=True,
                 )
+        late_wd = deal(cand_w, U32, 4, "late_wd", slice(2, PACK), tag="lo11")
+        late_sd = deal(cand_s, U8, 16, "late_sd", slice(2, PACK), tag="mn11")
+        a_late = [ps.tile([P, S], F32, name=f"a_late{e}", tag=f"y_ps{e}") for e in range(2)]
+        for e in range(2):
+            nc.tensor.matmul_mx(
+                out=a_late[e][:],
+                lhsT=late_wd[:, P * e : P * (e + 1)].bitcast(FP8X4),
+                lhsT_scale=late_sd[:, P * e : P * (e + 1)],
+                rhs=z_w[:].bitcast(FP8X4),
+                rhs_scale=z_s[:],
+                start=True,
+                stop=True,
+            )
 
         g3 = tile([P, PACK, S], F32, "g3")
         g4 = tile([P, PACK, S], F32, "g4")
@@ -195,42 +208,36 @@ def tile_picked_cdswclampbgmid_none_po_kernel(
             nc.scalar.activation(out=g4[:, t, :], in_=b_win[t][:].indirect(n4_l[:]), func=COPY)
 
         for h in range(2):
-            cols = slice(HALF * h, HALF * (h + 1))
-            for t in range(PACK):
-                if (h, t) in ((0, 2), (0, 3), (1, 2), (1, 3)):
-                    nc.vector.tensor_copy(out=a_win[t][:, cols], in_=a_ps[h][t // 2][:, t % 2, :])
-                else:
-                    nc.scalar.copy(out=a_win[t][:, cols], in_=a_ps[h][t // 2][:, t % 2, :])
+            for t in range(2):
+                nc.scalar.copy(out=a_win[t][:, HALF * h : HALF * (h + 1)], in_=a_ps[h][t])
+        for t in range(2, PACK):
+            nc.vector.tensor_copy(out=a_win[t][:, :S], in_=a_late[t % 2][:])
 
         out_rows = out_0.rearrange("(p t) j -> p t j", t=PACK)
         out_words = out_1[0].rearrange("p n t -> p (n t)")
         o_w = tile([P, S], U32, "o_w")
         o_s = tile([P, S], U8, "o_s")
+        res = tile([P, PACK, S], F32, "res")
+        for t in range(PACK):
+            g2 = tile([P, S], F32, f"g2{t}")
+            nc.scalar.activation(out=g2[:], in_=a_win[t][:].indirect(n2_l[:]), func=COPY)
+            diff = tile([P, S], F32, f"diff{t}")
+            nc.vector.scalar_tensor_tensor(
+                out=diff[:], in0=g2[:], scalar=-0.5, in1=a_win[t][:, :S], op0=ALU.mult, op1=ALU.add
+            )
+            low = tile([P, S], F32, f"low{t}")
+            nc.vector.scalar_tensor_tensor(
+                out=low[:], in0=diff[:], scalar=0.0625, in1=g3[:, t, :], op0=ALU.mult, op1=ALU.min
+            )
+            nc.vector.tensor_tensor(out=res[:, t, :], in0=low[:], in1=g4[:, t, :], op=ALU.max)
+            nc.sync.dma_start(out=out_rows[:, t, :], in_=res[:, t, :])
         for h in range(2):
             cols = slice(HALF * h, HALF * (h + 1))
-            res = tile([P, PACK, HALF], F32, f"res{h}")
-            for q in range(2):
-                pair = slice(2 * q, 2 * q + 2)
-                g2 = tile([P, 2, HALF], F32, f"g2{h}{q}")
-                for e in range(2):
-                    nc.scalar.activation(
-                        out=g2[:, e, :], in_=a_win[2 * q + e][:].indirect(n2_l[:, 8 * h : 8 * (h + 1)]), func=COPY
-                    )
-                diff = tile([P, 2, HALF], F32, f"diff{h}{q}")
-                nc.vector.scalar_tensor_tensor(
-                    out=diff[:], in0=g2[:], scalar=-0.5, in1=a_ps[h][q][:], op0=ALU.mult, op1=ALU.add
-                )
-                low = tile([P, 2, HALF], F32, f"low{h}{q}")
-                nc.vector.scalar_tensor_tensor(
-                    out=low[:], in0=diff[:], scalar=0.0625, in1=g3[:, pair, cols], op0=ALU.mult, op1=ALU.min
-                )
-                nc.vector.tensor_tensor(out=res[:, pair, :], in0=low[:], in1=g4[:, pair, cols], op=ALU.max)
-                nc.sync.dma_start(out=out_rows[:, pair, cols], in_=res[:, pair, :])
             o_bf = tile([P, HALF, PACK], BF16, f"o_bf{h}")
             if h == 0:
-                nc.scalar.copy(out=woven(o_bf), in_=by_runs(res))
+                nc.scalar.copy(out=o_bf[:], in_=by_column(res[:, :, cols]))
             else:
-                nc.vector.tensor_copy(out=woven(o_bf), in_=by_runs(res))
+                nc.vector.tensor_copy(out=o_bf[:], in_=by_column(res[:, :, cols]))
             nc.vector.quantize_mx(
                 out=o_w[:, cols].bitcast(FP8X4), scales=o_s[:, cols], in_=o_bf[:].rearrange("p j t -> p (j t)")
             )

@@ -21,6 +21,7 @@ PACK = 4
 HALF = S // 2
 Y_WINDOW = 528
 B_WINDOW = 512
+ROUND_SPLIT = 80
 
 
 def tile_picked_cdswclampbgmid_none_po_kernel(
@@ -53,7 +54,11 @@ def tile_picked_cdswclampbgmid_none_po_kernel(
         x_w = tile([P, T], U32, "x_w")
         nc.sync.dma_start(out=x_w[:].bitcast(I32), in_=x_words[0].rearrange("p n t -> p (n t)").bitcast(I32))
         w1_sc = tile([P, H], U8, "w1_sc")
-        load_scale_rows(w1_sc, w1_scales)
+        nc.vector.memset(w1_sc[:].bitcast(I32), 0)
+        for q in range(4):
+            nc.sync.dma_start(
+                out=w1_sc[32 * q : 32 * q + 4, :].bitcast(I32), in_=w1_scales[0][4 * q : 4 * q + 4, :].bitcast(I32)
+            )
         n1_l = load_list(n1, "n1_l")
         cand_l = load_list(cand, "cand_l")
         gs_t = tile([P, 1, PACK], F32, "gs_t")
@@ -96,13 +101,13 @@ def tile_picked_cdswclampbgmid_none_po_kernel(
             in_=w1_w[:].rearrange("p (m t b) -> p t m b", t=PACK, b=2),
         )
         xq_w = pick(x_w, offs_l, S, U32, "xq_w")
-        w1_sd = deal(w1_sc, U8, 16, "w1_sd")
+        w1_sd = [deal(w1_sc, U8, 16, "w1_sd0", slice(0, 1)), deal(w1_sc, U8, 16, "w1_sd1", slice(1, PACK))]
         y_ps = [ps.tile([P, 2, S], F32, name=f"y_ps{q}") for q in range(2)]
         for t in range(PACK):
             nc.tensor.matmul_mx(
                 out=y_ps[t // 2][:, t % 2, :],
                 lhsT=w1_wd[:, 2 * P * t : 2 * P * (t + 1)].bitcast(FP4X4),
-                lhsT_scale=w1_sd[:, P * t : P * (t + 1)],
+                lhsT_scale=w1_sd[0][:] if t == 0 else w1_sd[1][:, P * (t - 1) : P * t],
                 rhs=xq_w[:].bitcast(FP8X4),
                 rhs_scale=xq_s[:],
                 start=True,
@@ -201,15 +206,16 @@ def tile_picked_cdswclampbgmid_none_po_kernel(
             )
 
         g3 = tile([P, PACK, S], F32, "g3")
-        g4 = tile([P, PACK, S], F32, "g4")
+        g4 = [tile([P, S], F32, f"g4{t}") for t in range(2)]
         for t in range(PACK):
             nc.scalar.copy(out=b_win[t][:, :S], in_=b_ps[t // 2][:, t % 2, :])
             nc.scalar.activation(out=g3[:, t, :], in_=b_win[t][:].indirect(n3_l[:]), func=COPY)
-            nc.scalar.activation(out=g4[:, t, :], in_=b_win[t][:].indirect(n4_l[:]), func=COPY)
+            if t < 2:
+                nc.scalar.activation(out=g4[t][:], in_=b_win[t][:].indirect(n4_l[:]), func=COPY)
 
         for h in range(2):
             for t in range(2):
-                nc.scalar.copy(out=a_win[t][:, HALF * h : HALF * (h + 1)], in_=a_ps[h][t])
+                nc.vector.tensor_copy(out=a_win[t][:, HALF * h : HALF * (h + 1)], in_=a_ps[h][t])
         for t in range(2, PACK):
             nc.vector.tensor_copy(out=a_win[t][:, :S], in_=a_late[t % 2][:])
 
@@ -218,6 +224,12 @@ def tile_picked_cdswclampbgmid_none_po_kernel(
         o_w = tile([P, S], U32, "o_w")
         o_s = tile([P, S], U8, "o_s")
         res = tile([P, PACK, S], F32, "res")
+        lows = []
+
+        def finish(t):
+            nc.vector.tensor_tensor(out=res[:, t, :], in0=lows[t][:], in1=g4[t][:], op=ALU.max)
+            nc.sync.dma_start(out=out_rows[:, t, :], in_=res[:, t, :])
+
         for t in range(PACK):
             g2 = tile([P, S], F32, f"g2{t}")
             nc.scalar.activation(out=g2[:], in_=a_win[t][:].indirect(n2_l[:]), func=COPY)
@@ -229,21 +241,18 @@ def tile_picked_cdswclampbgmid_none_po_kernel(
             nc.vector.scalar_tensor_tensor(
                 out=low[:], in0=diff[:], scalar=0.0625, in1=g3[:, t, :], op0=ALU.mult, op1=ALU.min
             )
-            nc.vector.tensor_tensor(out=res[:, t, :], in0=low[:], in1=g4[:, t, :], op=ALU.max)
-            nc.sync.dma_start(out=out_rows[:, t, :], in_=res[:, t, :])
-        for h in range(2):
-            cols = slice(HALF * h, HALF * (h + 1))
-            o_bf = tile([P, HALF, PACK], BF16, f"o_bf{h}")
-            if h == 0:
-                nc.scalar.copy(out=o_bf[:], in_=by_column(res[:, :, cols]))
-            else:
-                nc.vector.tensor_copy(out=o_bf[:], in_=by_column(res[:, :, cols]))
-            nc.vector.quantize_mx(
-                out=o_w[:, cols].bitcast(FP8X4), scales=o_s[:, cols], in_=o_bf[:].rearrange("p j t -> p (j t)")
-            )
-            nc.sync.dma_start(
-                out=out_words[:, 4 * HALF * h : 4 * HALF * (h + 1)].bitcast(I32), in_=o_w[:, cols].bitcast(I32)
-            )
+            lows.append(low)
+            if t < 2:
+                finish(t)
+        for t in range(2, PACK):
+            g4.append(tile([P, S], F32, f"g4{t}", tag=f"g2{t - 2}"))
+            nc.scalar.activation(out=g4[t][:], in_=b_win[t][:].indirect(n4_l[:]), func=COPY)
+            finish(t)
+        o_bf = tile([P, S, PACK], BF16, "o_bf")
+        nc.scalar.copy(out=o_bf[:, :ROUND_SPLIT, :], in_=by_column(res[:, :, :ROUND_SPLIT]))
+        nc.vector.tensor_copy(out=o_bf[:, ROUND_SPLIT:, :], in_=by_column(res[:, :, ROUND_SPLIT:]))
+        nc.vector.quantize_mx(out=o_w[:].bitcast(FP8X4), scales=o_s[:], in_=o_bf[:].rearrange("p j t -> p (j t)"))
+        nc.sync.dma_start(out=out_words.bitcast(I32), in_=o_w[:].bitcast(I32))
         for q in range(4):
             queue = nc.sync if q % 2 == 0 else nc.scalar
             queue.dma_start(

@@ -61,8 +61,8 @@ def tile_picked_cdswclampbgmid_none_po_kernel(
             )
         n1_l = load_list(n1, "n1_l")
         cand_l = load_list(cand, "cand_l")
-        gs_t = tile([P, 1, PACK], F32, "gs_t")
-        nc.sync.dma_start(out=gs_t[:], in_=gs.rearrange("(p t) o -> p o t", t=PACK))
+        gs_t = tile([P, 1, PACK, 1], F32, "gs_t")
+        nc.sync.dma_start(out=gs_t[:, 0, :, :], in_=gs.rearrange("(p t) o -> p t o", t=PACK))
         wb_raw = tile([P, PACK, S], F32, "wb_raw")
         nc.sync.dma_start(out=wb_raw[:], in_=wb.rearrange("(p t) j -> p t j", t=PACK))
         n3_l = load_list(n3, "n3_l")
@@ -82,6 +82,11 @@ def tile_picked_cdswclampbgmid_none_po_kernel(
             nc.vector.tensor_copy(out=dst[:], in_=table[:].indirect(lst[:]))
             return dst
 
+        def pick_dealt(lst, name, tag=None):
+            dst = tile([P, C], U32, name, tag)
+            nc.vector.tensor_copy(out=dst[:].rearrange("p (t m) -> p m t", t=PACK), in_=x_w[:].indirect(lst[:]))
+            return dst
+
         def deal(src, dtype, run, name, slots=slice(0, PACK), tag=None):
             count = slots.stop - slots.start
             dst = tile([P, count * P], dtype, name, tag)
@@ -91,8 +96,11 @@ def tile_picked_cdswclampbgmid_none_po_kernel(
             )
             return dst
 
-        def by_column(src):
-            return src[:].rearrange("p t j -> p j t")
+        def woven(dst):
+            return dst.rearrange("p (c i) t -> p c t i", i=4)
+
+        def by_runs(src):
+            return src.rearrange("p t (c i) -> p c t i", i=4)
 
         xq_s = pick(x_sc, offs_l, S, U8, "xq_s")
         w1_wd = tile([P, 2 * H], U8, "w1_wd")
@@ -116,13 +124,12 @@ def tile_picked_cdswclampbgmid_none_po_kernel(
             nc.scalar.copy(out=y_win[t][:, :S], in_=y_ps[t // 2][:, t % 2, :])
 
         cb_s = pick(x_sc, cb_l, C, U8, "cb_s")
-        cb_w = pick(x_w, cb_l, C, U32, "cb_w", tag="w1_sc")
+        cb_wd = pick_dealt(cb_l, "cb_wd", tag="w1_sc")
         cb_sd = deal(cb_s, U8, 16, "cb_sd")
-        cb_wd = deal(cb_w, U32, 4, "cb_wd")
         wb_bf = tile([P, S, PACK], BF16, "wb_bf")
-        nc.vector.tensor_copy(out=wb_bf[:], in_=by_column(wb_raw))
+        nc.vector.tensor_copy(out=woven(wb_bf[:]), in_=by_runs(wb_raw[:]))
         cand_s = pick(x_sc, cand_l, C, U8, "cand_s")
-        cand_w = pick(x_w, cand_l, C, U32, "cand_w")
+        cand_wd = pick_dealt(cand_l, "cand_wd")
         wb_w = tile([P, S], U32, "wb_w")
         wb_s = tile([P, S], U8, "wb_s")
         nc.vector.quantize_mx(out=wb_w[:].bitcast(FP8X4), scales=wb_s[:], in_=wb_bf[:].rearrange("p j t -> p (j t)"))
@@ -137,7 +144,6 @@ def tile_picked_cdswclampbgmid_none_po_kernel(
                 start=True,
                 stop=True,
             )
-        cand_wd = deal(cand_w, U32, 4, "cand_wd", slice(0, 2))
         cand_sd = deal(cand_s, U8, 16, "cand_sd", slice(0, 2))
         z_w = tile([P, S], U32, "z_w")
         z_s = tile([P, S], U8, "z_s")
@@ -173,9 +179,9 @@ def tile_picked_cdswclampbgmid_none_po_kernel(
             )
             z_bf = tile([P, HALF, PACK], BF16, f"z_bf{h}")
             nc.vector.tensor_tensor(
-                out=z_bf[:],
-                in0=by_column(u),
-                in1=gs_t[:].to_broadcast([P, HALF, PACK]),
+                out=woven(z_bf[:]),
+                in0=by_runs(u[:]),
+                in1=gs_t[:].to_broadcast([P, HALF // 4, PACK, 4]),
                 op=ALU.mult,
             )
             nc.vector.quantize_mx(
@@ -191,13 +197,12 @@ def tile_picked_cdswclampbgmid_none_po_kernel(
                     start=True,
                     stop=True,
                 )
-        late_wd = deal(cand_w, U32, 4, "late_wd", slice(2, PACK), tag="lo11")
         late_sd = deal(cand_s, U8, 16, "late_sd", slice(2, PACK), tag="mn11")
         a_late = [ps.tile([P, S], F32, name=f"a_late{e}", tag=f"y_ps{e}") for e in range(2)]
         for e in range(2):
             nc.tensor.matmul_mx(
                 out=a_late[e][:],
-                lhsT=late_wd[:, P * e : P * (e + 1)].bitcast(FP8X4),
+                lhsT=cand_wd[:, P * (2 + e) : P * (3 + e)].bitcast(FP8X4),
                 lhsT_scale=late_sd[:, P * e : P * (e + 1)],
                 rhs=z_w[:].bitcast(FP8X4),
                 rhs_scale=z_s[:],
@@ -249,8 +254,8 @@ def tile_picked_cdswclampbgmid_none_po_kernel(
             nc.scalar.activation(out=g4[t][:], in_=b_win[t][:].indirect(n4_l[:]), func=COPY)
             finish(t)
         o_bf = tile([P, S, PACK], BF16, "o_bf")
-        nc.scalar.copy(out=o_bf[:, :ROUND_SPLIT, :], in_=by_column(res[:, :, :ROUND_SPLIT]))
-        nc.vector.tensor_copy(out=o_bf[:, ROUND_SPLIT:, :], in_=by_column(res[:, :, ROUND_SPLIT:]))
+        nc.scalar.copy(out=woven(o_bf[:, :ROUND_SPLIT, :]), in_=by_runs(res[:, :, :ROUND_SPLIT]))
+        nc.vector.tensor_copy(out=woven(o_bf[:, ROUND_SPLIT:, :]), in_=by_runs(res[:, :, ROUND_SPLIT:]))
         nc.vector.quantize_mx(out=o_w[:].bitcast(FP8X4), scales=o_s[:], in_=o_bf[:].rearrange("p j t -> p (j t)"))
         nc.sync.dma_start(out=out_words.bitcast(I32), in_=o_w[:].bitcast(I32))
         for q in range(4):

from contextlib import ExitStack

import concourse.mybir as mybir

K, T, S, H, W, C = 512, 2048, 256, 512, 1024, 512
FLOPS = 2 * K * S * (H + 2 * C)

F32 = mybir.dt.float32
BF16 = mybir.dt.bfloat16
I32 = mybir.dt.int32
U32 = mybir.dt.uint32
U16 = mybir.dt.uint16
U8 = mybir.dt.uint8
FP8X4 = mybir.dt.float8_e4m3fn_x4
FP4X4 = mybir.dt.float4_e2m1fn_x4
COPY = mybir.ActivationFunctionType.Copy
ALU = mybir.AluOpType

P = 128
PACK = 4
HALF = S // 2
Y_WINDOW = 528
B_WINDOW = 512
ROUND_SPLIT = 80


def tile_picked_cdswclampbgmid_none_po_kernel(
    tc, x_words, x_scales, w1_words, w1_scales, gs, wb, offs, n1, cand, cb, n2, n3, n4, out_0, out_1, out_2
):
    nc = tc.nc
    with ExitStack() as ctx:
        sb = ctx.enter_context(tc.tile_pool(name="sb", bufs=1))
        ps = ctx.enter_context(tc.psum_pool(name="ps", bufs=1))

        def tile(shape, dtype, name, tag=None):
            return sb.tile(shape, dtype, name=name, tag=tag or name, align_bytes=64)

        def load_list(src, name):
            dst = tile([P, src.shape[1]], U16, name)
            nc.sync.dma_start(dst[:], src)
            return dst

        def load_scale_rows(dst, src):
            for q in range(4):
                rows = src[0][4 * q : 4 * q + 4, :].bitcast(I32)
                nc.sync.dma_start(out=dst[32 * q : 32 * (q + 1), :].bitcast(I32), in_=rows.partition_broadcast(8))

        x_sc = tile([P, T], U8, "x_sc")
        load_scale_rows(x_sc, x_scales)
        offs_l = load_list(offs, "offs_l")
        cb_l = load_list(cb, "cb_l")
        w1_w = tile([P, 2 * H], U8, "w1_w")
        nc.sync.dma_start(out=w1_w[:].bitcast(I32), in_=w1_words[0].bitcast(I32))
        x_w = tile([P, T], U32, "x_w")
        nc.sync.dma_start(out=x_w[:].bitcast(I32), in_=x_words[0].rearrange("p n t -> p (n t)").bitcast(I32))
        w1_sc = tile([P, H], U8, "w1_sc")
        nc.vector.memset(w1_sc[:].bitcast(I32), 0)
        for q in range(4):
            nc.sync.dma_start(
                out=w1_sc[32 * q : 32 * q + 4, :].bitcast(I32), in_=w1_scales[0][4 * q : 4 * q + 4, :].bitcast(I32)
            )
        n1_l = load_list(n1, "n1_l")
        cand_l = load_list(cand, "cand_l")
        gs_t = tile([P, 1, PACK, 1], F32, "gs_t")
        nc.sync.dma_start(out=gs_t[:, 0, :, :], in_=gs.rearrange("(p t) o -> p t o", t=PACK))
        wb_raw = tile([P, PACK, S], F32, "wb_raw")
        nc.sync.dma_start(out=wb_raw[:], in_=wb.rearrange("(p t) j -> p t j", t=PACK))
        n3_l = load_list(n3, "n3_l")
        n4_l = load_list(n4, "n4_l")
        n2_l = load_list(n2, "n2_l")

        y_win = [tile([P, Y_WINDOW], F32, f"y_win{t}") for t in range(PACK)]
        a_win = [tile([P, B_WINDOW], F32, f"a_win{t}") for t in range(PACK)]
        b_win = [tile([P, B_WINDOW], F32, f"b_win{t}") for t in range(PACK)]
        for win in y_win + b_win:
            nc.vector.memset(win[:, S:], 0.0)
        for win in a_win:
            nc.gpsimd.memset(win[:, S:], 0.0)

        def pick(table, lst, n, dtype, name, tag=None):
            dst = tile([P, n], dtype, name, tag)
            nc.vector.tensor_copy(out=dst[:], in_=table[:].indirect(lst[:]))
            return dst

        def pick_dealt(lst, name, tag=None):
            dst = tile([P, C], U32, name, tag)
            nc.vector.tensor_copy(out=dst[:].rearrange("p (t m) -> p m t", t=PACK), in_=x_w[:].indirect(lst[:]))
            return dst

        def deal(src, dtype, run, name, slots=slice(0, PACK), tag=None):
            count = slots.stop - slots.start
            dst = tile([P, count * P], dtype, name, tag)
            nc.vector.tensor_copy(
                out=dst[:].rearrange("p (t c i) -> p c t i", t=count, i=run),
                in_=src[:].rearrange("p (c i t) -> p c t i", t=PACK, i=run)[:, :, slots, :],
            )
            return dst

        def woven(dst):
            return dst.rearrange("p (c i) t -> p c t i", i=4)

        def by_runs(src):
            return src.rearrange("p t (c i) -> p c t i", i=4)

        xq_s = pick(x_sc, offs_l, S, U8, "xq_s")
        w1_wd = tile([P, 2 * H], U8, "w1_wd")
        nc.vector.tensor_copy(
            out=w1_wd[:].rearrange("p (t m b) -> p t m b", t=PACK, b=2),
            in_=w1_w[:].rearrange("p (m t b) -> p t m b", t=PACK, b=2),
        )
        xq_w = pick(x_w, offs_l, S, U32, "xq_w")
        w1_sd = [deal(w1_sc, U8, 16, "w1_sd0", slice(0, 1)), deal(w1_sc, U8, 16, "w1_sd1", slice(1, PACK))]
        y_ps = [ps.tile([P, 2, S], F32, name=f"y_ps{q}") for q in range(2)]
        for t in range(PACK):
            nc.tensor.matmul_mx(
                out=y_ps[t // 2][:, t % 2, :],
                lhsT=w1_wd[:, 2 * P * t : 2 * P * (t + 1)].bitcast(FP4X4),
                lhsT_scale=w1_sd[0][:] if t == 0 else w1_sd[1][:, P * (t - 1) : P * t],
                rhs=xq_w[:].bitcast(FP8X4),
                rhs_scale=xq_s[:],
                start=True,
                stop=True,
            )
            nc.scalar.copy(out=y_win[t][:, :S], in_=y_ps[t // 2][:, t % 2, :])

        cb_s = pick(x_sc, cb_l, C, U8, "cb_s")
        cb_wd = pick_dealt(cb_l, "cb_wd", tag="w1_sc")
        cb_sd = deal(cb_s, U8, 16, "cb_sd")
        wb_bf = tile([P, S, PACK], BF16, "wb_bf")
        nc.vector.tensor_copy(out=woven(wb_bf[:]), in_=by_runs(wb_raw[:]))
        cand_s = pick(x_sc, cand_l, C, U8, "cand_s")
        cand_wd = pick_dealt(cand_l, "cand_wd")
        wb_w = tile([P, S], U32, "wb_w")
        wb_s = tile([P, S], U8, "wb_s")
        nc.vector.quantize_mx(out=wb_w[:].bitcast(FP8X4), scales=wb_s[:], in_=wb_bf[:].rearrange("p j t -> p (j t)"))
        b_ps = [ps.tile([P, 2, S], F32, name=f"b_ps{q}") for q in range(2)]
        for t in range(PACK):
            nc.tensor.matmul_mx(
                out=b_ps[t // 2][:, t % 2, :],
                lhsT=cb_wd[:, P * t : P * (t + 1)].bitcast(FP8X4),
                lhsT_scale=cb_sd[:, P * t : P * (t + 1)],
                rhs=wb_w[:].bitcast(FP8X4),
                rhs_scale=wb_s[:],
                start=True,
                stop=True,
            )
        cand_sd = deal(cand_s, U8, 16, "cand_sd", slice(0, 2))
        z_w = tile([P, S], U32, "z_w")
        z_s = tile([P, S], U8, "z_s")

        a_first = ps.tile([P, 2, HALF], F32, name="a_first")
        a_ps = [[a_first[:, t, :] for t in range(2)], [ps.tile([P, HALF], F32, name=f"a_second{t}")[:] for t in range(2)]]
        for h in range(2):
            cols = slice(HALF * h, HALF * (h + 1))
            u = tile([P, PACK, HALF], F32, f"u{h}")
            top = tile([P, PACK, HALF], F32, f"top{h}")
            mx = tile([P, PACK, HALF], F32, f"mx{h}")
            for q in range(2):
                pair = slice(2 * q, 2 * q + 2)
                mb = tile([P, 2, 4 * HALF], F32, f"mb{h}{q}")
                for e in range(2):
                    t = 2 * q + e
                    nc.scalar.activation(out=mb[:, e, :], in_=y_win[t][:].indirect(n1_l[:, 32 * h : 32 * (h + 1)]), func=COPY)
                members = mb[:].rearrange("p e (j m) -> p (e j) m", m=4)
                lo = tile([P, S, 2], F32, f"lo{h}{q}")
                hi = tile([P, S, 2], F32, f"hi{h}{q}")
                mn = tile([P, 2, HALF], F32, f"mn{h}{q}")
                nc.vector.tensor_tensor(out=lo[:], in0=members[:, :, 0:2], in1=members[:, :, 2:4], op=ALU.min)
                nc.vector.tensor_tensor(out=hi[:], in0=members[:, :, 0:2], in1=members[:, :, 2:4], op=ALU.max)
                nc.vector.tensor_tensor(
                    out=mn[:].rearrange("p e j -> p (e j)"), in0=lo[:, :, 0], in1=lo[:, :, 1], op=ALU.min
                )
                nc.vector.tensor_tensor(
                    out=mx[:, pair, :].rearrange("p e j -> p (e j)"), in0=hi[:, :, 0], in1=hi[:, :, 1], op=ALU.max
                )
                nc.vector.tensor_tensor(out=top[:, pair, :], in0=y_ps[q][:, :, cols], in1=mn[:], op=ALU.max)
            nc.vector.scalar_tensor_tensor(
                out=u[:], in0=mx[:], scalar=-0.5, in1=top[:], op0=ALU.mult, op1=ALU.add
            )
            z_bf = tile([P, HALF, PACK], BF16, f"z_bf{h}")
            nc.vector.tensor_tensor(
                out=woven(z_bf[:]),
                in0=by_runs(u[:]),
                in1=gs_t[:].to_broadcast([P, HALF // 4, PACK, 4]),
                op=ALU.mult,
            )
            nc.vector.quantize_mx(
                out=z_w[:, cols].bitcast(FP8X4), scales=z_s[:, cols], in_=z_bf[:].rearrange("p j t -> p (j t)")
            )
            for t in range(2):
                nc.tensor.matmul_mx(
                    out=a_ps[h][t],
                    lhsT=cand_wd[:, P * t : P * (t + 1)].bitcast(FP8X4),
                    lhsT_scale=cand_sd[:, P * t : P * (t + 1)],
                    rhs=z_w[:, cols].bitcast(FP8X4),
                    rhs_scale=z_s[:, cols],
                    start=True,
                    stop=True,
                )
        late_sd = deal(cand_s, U8, 16, "late_sd", slice(2, PACK), tag="mn11")
        a_late = [ps.tile([P, S], F32, name=f"a_late{e}", tag=f"y_ps{e}") for e in range(2)]
        for e in range(2):
            nc.tensor.matmul_mx(
                out=a_late[e][:],
                lhsT=cand_wd[:, P * (2 + e) : P * (3 + e)].bitcast(FP8X4),
                lhsT_scale=late_sd[:, P * e : P * (e + 1)],
                rhs=z_w[:].bitcast(FP8X4),
                rhs_scale=z_s[:],
                start=True,
                stop=True,
            )

        g3 = tile([P, PACK, S], F32, "g3")
        g4 = [tile([P, S], F32, f"g4{t}") for t in range(2)]
        for t in range(PACK):
            nc.scalar.copy(out=b_win[t][:, :S], in_=b_ps[t // 2][:, t % 2, :])
            nc.scalar.activation(out=g3[:, t, :], in_=b_win[t][:].indirect(n3_l[:]), func=COPY)
            if t < 2:
                nc.scalar.activation(out=g4[t][:], in_=b_win[t][:].indirect(n4_l[:]), func=COPY)

        for h in range(2):
            for t in range(2):
                nc.vector.tensor_copy(out=a_win[t][:, HALF * h : HALF * (h + 1)], in_=a_ps[h][t])
        for t in range(2, PACK):
            nc.vector.tensor_copy(out=a_win[t][:, :S], in_=a_late[t % 2][:])

        out_rows = out_0.rearrange("(p t) j -> p t j", t=PACK)
        out_words = out_1[0].rearrange("p n t -> p (n t)")
        o_w = tile([P, S], U32, "o_w")
        o_s = tile([P, S], U8, "o_s")
        res = tile([P, PACK, S], F32, "res")
        lows = []

        def finish(t):
            nc.vector.tensor_tensor(out=res[:, t, :], in0=lows[t][:], in1=g4[t][:], op=ALU.max)
            nc.sync.dma_start(out=out_rows[:, t, :], in_=res[:, t, :])

        for t in range(PACK):
            g2 = tile([P, S], F32, f"g2{t}")
            nc.scalar.activation(out=g2[:], in_=a_win[t][:].indirect(n2_l[:]), func=COPY)
            diff = tile([P, S], F32, f"diff{t}")
            nc.vector.scalar_tensor_tensor(
                out=diff[:], in0=g2[:], scalar=-0.5, in1=a_win[t][:, :S], op0=ALU.mult, op1=ALU.add
            )
            low = tile([P, S], F32, f"low{t}")
            nc.vector.scalar_tensor_tensor(
                out=low[:], in0=diff[:], scalar=0.0625, in1=g3[:, t, :], op0=ALU.mult, op1=ALU.min
            )
            lows.append(low)
            if t < 2:
                finish(t)
        for t in range(2, PACK):
            g4.append(tile([P, S], F32, f"g4{t}", tag=f"g2{t - 2}"))
            nc.scalar.activation(out=g4[t][:], in_=b_win[t][:].indirect(n4_l[:]), func=COPY)
            finish(t)
        o_bf = tile([P, S, PACK], BF16, "o_bf")
        nc.scalar.copy(out=woven(o_bf[:, :ROUND_SPLIT, :]), in_=by_runs(res[:, :, :ROUND_SPLIT]))
        nc.vector.tensor_copy(out=woven(o_bf[:, ROUND_SPLIT:, :]), in_=by_runs(res[:, :, ROUND_SPLIT:]))
        nc.vector.quantize_mx(out=o_w[:].bitcast(FP8X4), scales=o_s[:], in_=o_bf[:].rearrange("p j t -> p (j t)"))
        nc.sync.dma_start(out=out_words.bitcast(I32), in_=o_w[:].bitcast(I32))
        for q in range(4):
            queue = nc.sync if q % 2 == 0 else nc.scalar
            queue.dma_start(
                out=out_2[0][4 * q : 4 * q + 4, :].bitcast(I32), in_=o_s[32 * q : 32 * q + 4, :].bitcast(I32)
            )
